import numpy as np
import ml_dtypes


def mxq(x, axis, fmt="e4m3"):
    dtype, down = {"e4m3": (ml_dtypes.float8_e4m3fn, 7), "e5m2": (ml_dtypes.float8_e5m2, 14)}[fmt]
    v = np.moveaxis(np.asarray(x, np.float32).astype(ml_dtypes.bfloat16).astype(np.float64), axis, -1)
    blocks = v.reshape(v.shape[:-1] + (-1, 32))
    amax = np.abs(blocks).max(-1, keepdims=True)
    byte = np.maximum(np.where(amax > 0, np.frexp(amax)[1] - 1 + 127, 0) - down, 1)
    scale = np.exp2(byte - 127.0)
    codes = (blocks / scale).astype(np.float32).astype(dtype).astype(np.float64)
    return np.moveaxis((codes * scale).reshape(v.shape), -1, axis)


WIDE = False


def mx_kscale(k):
    if not WIDE:
        return np.ones(k)
    levels = np.array([30, -30])
    if k % 512:
        return np.exp2(np.random.permutation(np.resize(levels, k // 32))).repeat(32)
    a = np.empty((k // 512, 16))
    for p in range(k // 512):
        a[p, :8] = np.random.permutation(np.resize(levels, 8))
        for g in range(8):
            far = levels[np.abs(levels - a[p, g]) >= 10]
            a[p, g + 8] = far[np.random.randint(len(far))]
    return np.exp2(a.ravel()).repeat(32)


def f64(x):
    return np.asarray(x).astype(np.float64)


def striped(idx):
    return np.tile(np.asarray(idx).reshape(-1, 16).T, (8, 1)).astype(np.uint16)


def unstriped(offs):
    return offs[:16].T.reshape(-1).astype(np.int64)


def striped8(idx):
    return np.asarray(idx).reshape(8, -1, 16).transpose(0, 2, 1).reshape(128, -1).astype(np.uint16)


def unstriped8(offs):
    return offs.reshape(8, 16, -1).transpose(0, 2, 1).reshape(8, -1).astype(np.int64)


def pick8(x, idx, run):
    r = np.arange(len(x))
    return x[r[:, None], idx[r % (8 * run) // run]]


E2M1 = np.array([0.0, 0.5, 1.0, 1.5, 2.0, 3.0, 4.0, 6.0, -0.0, -0.5, -1.0, -1.5, -2.0, -3.0, -4.0, -6.0])


def pack_weight(w, fmt):
    k, n = w.shape
    w = f64(np.asarray(w, np.float32).astype(ml_dtypes.bfloat16)).reshape(k // 32, 32, n)
    amax = np.abs(w).max(1)
    if fmt in ("e4m3", "e5m2"):
        byte = np.frexp(amax)[1] - 1 + 127 - (7 if fmt == "e4m3" else 14)
    else:
        mant, ex = np.frexp(amax / 6.0)
        byte = np.where(mant > 0.5, ex, ex - 1) + 127
    byte = np.clip(np.where(amax > 0, byte, 1), 1, 254)
    scaled = (w * np.exp2(127.0 - byte)[:, None, :]).reshape(k, n).astype(np.float32)
    by_word = np.ascontiguousarray(scaled.reshape(k // 512, 128, 4, n).transpose(0, 1, 3, 2))
    if fmt in ("e4m3", "e5m2"):
        words = by_word.astype(ml_dtypes.float8_e4m3fn if fmt == "e4m3" else ml_dtypes.float8_e5m2).view(np.uint8)
    else:
        c = by_word.astype(ml_dtypes.float4_e2m1fn).view(np.uint8) & 0xF
        words = (c[..., 0::2] | (c[..., 1::2] << 4)).reshape(k // 512, 128, 2 * n)
    return np.ascontiguousarray(words), np.ascontiguousarray(byte.astype(np.uint8).reshape(k // 512, 16, n))


def unpack_weight(words, scales, fmt):
    g, _, n = scales.shape
    words = np.ascontiguousarray(words).reshape(g, 128, n, -1)
    if fmt in ("e4m3", "e5m2"):
        vals = words.view(ml_dtypes.float8_e4m3fn if fmt == "e4m3" else ml_dtypes.float8_e5m2).astype(np.float64)
    else:
        nib = np.empty((g, 128, n, 4), np.uint8)
        nib[..., 0::2] = words & 0xF
        nib[..., 1::2] = words >> 4
        vals = E2M1[nib]
    vals = vals * np.repeat(np.exp2(scales.astype(np.float64) - 127.0), 8, axis=1)[..., None]
    return vals.transpose(0, 1, 3, 2).reshape(g * 512, n)


def sigmoid(v):
    return 1.0 / (1.0 + np.exp(-v))


def sgn(shape):
    return np.random.uniform(0.5, 2.0, shape) * np.where(np.random.standard_normal(shape) < 0, -1.0, 1.0)


K, T, J, R, C, O, N, S, U, E = 512, 1024, 256, 512, 512, 256, 256, 1024, 128, 512


def setup_inputs():
    n = np.random.standard_normal
    idx = np.random.permutation(T)[:J]
    idx2 = np.stack([np.random.permutation(C)[:J] for _ in range(8)])
    idx3 = np.stack([np.random.permutation(C)[:O] for _ in range(8)])
    idx4 = np.stack([np.random.permutation(C)[:O] for _ in range(8)])
    idx5 = np.random.permutation(S)[:N]
    idx6 = np.random.permutation(O)[:U]
    idx7 = np.random.permutation(E)[:U]
    fk = mx_kscale(K)
    fr = mx_kscale(R)
    xtp = pack_weight(n((K, T)) / fk[:, None], "e2m1")
    wp = pack_weight(n((K, R)) * 1 / np.sqrt(K) * fk[:, None], "e5m2")
    vsp = pack_weight(n((R, S)) * 1 / np.sqrt(R) / fr[:, None], "e4m3")
    return {
        "xt_words": xtp[0],
        "xt_scales": xtp[1],
        "w_words": wp[0],
        "w_scales": wp[1],
        "sa": (np.random.uniform(0.5, 1.6, (R, 1)) * fr[:, None]).astype(np.float32),
        "sg": (sgn((R, 1))).astype(np.float32),
        "bg": (np.random.uniform(-2.0, 2.0, (R, 1))).astype(np.float32),
        "vs_words": vsp[0],
        "vs_scales": vsp[1],
        "so": (sgn((N, 1))).astype(np.float32),
        "offs": striped(idx),
        "offs2": striped8(idx2),
        "offs3": striped8(idx3),
        "offs4": striped8(idx4),
        "offs5": striped(idx5),
        "offs6": striped(idx6),
        "offs7": striped(idx7),
    }


def reference(xt_words, xt_scales, w_words, w_scales, sa, sg, bg, vs_words, vs_scales, so, offs, offs2, offs3, offs4, offs5, offs6, offs7):
    idx = unstriped(offs)
    idx2 = unstriped8(offs2)
    idx3 = unstriped8(offs3)
    idx4 = unstriped8(offs4)
    idx5 = unstriped(offs5)
    idx6 = unstriped(offs6)
    idx7 = unstriped(offs7)
    xtu = unpack_weight(xt_words, xt_scales, "e2m1")
    wu = unpack_weight(w_words, w_scales, "e5m2")
    vsu = unpack_weight(vs_words, vs_scales, "e4m3")
    xtidxg = xtu[:, idx]
    a = wu.T @ xtidxg
    pw = np.zeros((R, C))
    pw[np.arange(R)[:, None], idx2[np.arange(R) % 512 // 64]] = a
    hid = pick8(pw, idx3, 64) * f64(sa) * sigmoid(pick8(pw, idx4, 64) * f64(sg) + f64(bg))
    vsidx5g = vsu[:, idx5]
    hidq = mxq(hid, 0, "e5m2")
    p = vsidx5g.T @ hidq
    m0 = p[:, idx6] * f64(so)
    y = np.zeros((N, E))
    y[:, idx7] = m0
    return y

@@ -1,0 +1,182 @@
+from contextlib import ExitStack
+
+import concourse.mybir as mybir
+
+F32 = mybir.dt.float32
+BF16 = mybir.dt.bfloat16
+I32 = mybir.dt.int32
+U32 = mybir.dt.uint32
+U16 = mybir.dt.uint16
+U8 = mybir.dt.uint8
+E2M1X4 = mybir.dt.float4_e2m1fn_x4
+E4M3X4 = mybir.dt.float8_e4m3fn_x4
+E5M2X4 = mybir.dt.float8_e5m2_x4
+ACT = mybir.ActivationFunctionType
+
+P = 128
+PACK = 4
+K, T, J, R, C, O, N, S, U, E = 512, 1024, 256, 512, 512, 256, 256, 1024, 128, 512
+HALF = 128
+LIST_ROWS = 16
+QUADRANT = 32
+
+FLOPS = 2 * K * R * J + 2 * R * N * O
+
+
+def tile_list_gatedgroupboard_solo_store_postedout_kernel(
+    tc, xt_words, xt_scales, w_words, w_scales, sa, sg, bg, vs_words, vs_scales, so,
+    offs, offs2, offs3, offs4, offs5, offs6, offs7, out,
+):
+    nc = tc.nc
+    with ExitStack() as ctx:
+        lists = ctx.enter_context(tc.tile_pool(name="lists", bufs=1))
+        sb = ctx.enter_context(tc.tile_pool(name="sb", bufs=1))
+        reuse = ctx.enter_context(tc.tile_pool(name="reuse", bufs=1))
+        psum = ctx.enter_context(tc.psum_pool(name="psum", bufs=1))
+
+        def load_list(name, src):
+            t = lists.tile(list(src.shape), U16, name=name)
+            nc.sync.dma_start(t[:], src)
+            return t
+
+        def load_plane(plane, scales):
+            for q in range(4):
+                nc.sync.dma_start(
+                    plane[QUADRANT * q : QUADRANT * q + 4, :].bitcast(I32),
+                    scales[0, 4 * q : 4 * q + 4, :].bitcast(I32),
+                )
+
+        def half_of(lst, h):
+            return lst[:, h * HALF // LIST_ROWS : (h + 1) * HALF // LIST_ROWS]
+
+        xt_plane = sb.tile([P, T], U8, name="xt_plane")
+        w_plane = sb.tile([P, R], U8, name="w_plane")
+        vs_plane = sb.tile([P, S], U8, name="vs_plane")
+        boards = [sb.tile([P, C], F32, name=f"board{t}") for t in range(PACK)]
+        pages = [sb.tile([P, E], F32, name=f"page{n}") for n in range(N // P)]
+        nc.vector.memset(xt_plane[:].bitcast(I32), 0)
+        nc.vector.memset(w_plane[:].bitcast(I32), 0)
+        for board in boards:
+            nc.vector.memset(board[:], 0.0)
+
+        nc.gpsimd.memset(vs_plane[:].bitcast(I32), 0)
+        for page in pages:
+            nc.gpsimd.memset(page[:], 0.0)
+        w_rows = sb.tile([PACK, 4, R // 4], I32, name="w_rows")
+        nc.sync.dma_start(w_rows[:], w_scales[0].bitcast(I32).rearrange("(q r) c -> r q c", r=4))
+        idx = load_list("idx", offs)
+        xt_tab = sb.tile([P, T], U16, name="xt_tab")
+        nc.sync.dma_start(xt_tab[:].bitcast(I32), xt_words[0].bitcast(I32))
+        w_raw = sb.tile([P, R], I32, name="w_raw")
+        nc.sync.dma_start(w_raw[:], w_words[0].rearrange("p c b -> p (c b)").bitcast(I32))
+        load_plane(xt_plane, xt_scales)
+        idx2 = load_list("idx2", offs2)
+        idx4 = load_list("idx4", offs4)
+        idx3 = load_list("idx3", offs3)
+        sg_t = sb.tile([P, PACK], F32, name="sg_t")
+        bg_t = sb.tile([P, PACK], F32, name="bg_t")
+        sa_t = sb.tile([P, PACK], F32, name="sa_t")
+        for dst, src in ((sg_t, sg), (bg_t, bg), (sa_t, sa)):
+            nc.sync.dma_start(dst[:], src.rearrange("(p t) one -> p (t one)", t=PACK))
+        vs_tab = sb.tile([P, S], I32, name="vs_tab")
+        nc.sync.dma_start(vs_tab[:], vs_words[0].rearrange("p c b -> p (c b)").bitcast(I32))
+        idx5 = load_list("idx5", offs5)
+        load_plane(vs_plane, vs_scales)
+        idx6 = load_list("idx6", offs6)
+        idx7 = load_list("idx7", offs7)
+        so_t = sb.tile([P, N // P], F32, name="so_t")
+        with nc.allow_non_contiguous_dma(reason="one value a partition"):
+            nc.sync.dma_start(so_t[:], so.rearrange("(a p) one -> p (a one)", p=P))
+
+        for q in range(4):
+            nc.vector.tensor_copy(w_plane[QUADRANT * q : QUADRANT * q + 4, :].bitcast(I32), w_rows[:, q, :])
+        w_sc = sb.tile([P, PACK, P], U8, name="w_sc", align_bytes=64)
+        nc.vector.tensor_copy(
+            w_sc[:].rearrange("p t m -> p m t"), w_plane[:].rearrange("p (m t) -> p m t", t=PACK)
+        )
+        w_q = sb.tile([P, PACK, P], U32, name="w_q", align_bytes=64)
+        nc.scalar.copy(
+            w_q[:].rearrange("p t m -> p m t"), w_raw[:].bitcast(U32).rearrange("p (m t) -> p m t", t=PACK)
+        )
+
+        xg = sb.tile([P, J], U16, name="xg", align_bytes=64)
+        xg_sc = sb.tile([P, J], U8, name="xg_sc", align_bytes=64)
+        for h in range(2):
+            cols = slice(h * HALF, (h + 1) * HALF)
+            nc.vector.tensor_copy(xg[:, cols], xt_tab[:].indirect(half_of(idx, h)))
+            nc.vector.tensor_copy(xg_sc[:, cols], xt_plane[:].indirect(half_of(idx, h)))
+
+        a_sb = [sb.tile([P, J], F32, name=f"a_sb{t}") for t in range(PACK - 1)]
+        a_sb.append(reuse.tile([P, J], F32, name="a_last", offset=0, align_bytes=64))
+        steps = [(0, 0, 128), (0, 128, 256), (1, 0, 256), (2, 0, 256), (3, 0, 256)]
+        for i, (t, j0, j1) in enumerate(steps):
+            acc = psum.tile([P, j1 - j0], F32, name=f"bank{i}")
+            nc.tensor.matmul_mx(
+                out=acc[:],
+                lhsT=w_q[:, t, :].bitcast(E5M2X4), lhsT_scale=w_sc[:, t, :],
+                rhs=xg[:, j0:j1].bitcast(E2M1X4), rhs_scale=xg_sc[:, j0:j1],
+                start=True, stop=True,
+            )
+            nc.scalar.copy(a_sb[t][:, j0:j1], acc[:])
+        for t, j0, j1 in steps:
+            nc.vector.tensor_copy(
+                boards[t][:].indirect(idx2[:, j0 // LIST_ROWS : j1 // LIST_ROWS]), a_sb[t][:, j0:j1]
+            )
+
+        gate = sb.tile([P, PACK, O], F32, name="gate")
+        val = sb.tile([P, PACK, O], F32, name="val")
+        for t in range(PACK):
+            for o0, o1 in ((0, HALF), (HALF, O)) if t == PACK - 1 else ((0, O),):
+                entries = slice(o0 // LIST_ROWS, o1 // LIST_ROWS)
+                nc.scalar.activation(
+                    gate[:, t, o0:o1], boards[t][:].indirect(idx4[:, entries]), ACT.Sigmoid,
+                    bias=bg_t[:, t : t + 1], scale=sg_t[:, t : t + 1],
+                )
+                nc.scalar.activation(
+                    val[:, t, o0:o1], boards[t][:].indirect(idx3[:, entries]), ACT.Copy,
+                    scale=sa_t[:, t : t + 1],
+                )
+
+        vg = reuse.tile([P, N], U32, name="vg", offset=N, align_bytes=64)
+        vg_sc = reuse.tile([P, N], U8, name="vg_sc", offset=0, align_bytes=64)
+        nc.vector.tensor_copy(vg[:], vs_tab[:].bitcast(U32).indirect(idx5[:]))
+        nc.vector.tensor_copy(vg_sc[:], vs_plane[:].indirect(idx5[:]))
+
+        hid = [sb.tile([P, HALF, PACK], BF16, name=f"hid{h}", align_bytes=64) for h in range(2)]
+        hq = [sb.tile([P, HALF], U32, name=f"hq{h}", align_bytes=64) for h in range(2)]
+        hq_sc = [sb.tile([P, HALF], U8, name=f"hq_sc{h}", align_bytes=64) for h in range(2)]
+        for h in range(2):
+            nc.vector.tensor_tensor(
+                hid[h][:].rearrange("p (c i) t -> p c t i", i=4),
+                val[:, :, h * HALF : (h + 1) * HALF].rearrange("p t (c i) -> p c t i", i=4),
+                gate[:, :, h * HALF : (h + 1) * HALF].rearrange("p t (c i) -> p c t i", i=4),
+                mybir.AluOpType.mult,
+            )
+        for h in range(2):
+            nc.vector.quantize_mx(
+                out=hq[h][:].bitcast(E5M2X4), scales=hq_sc[h][:], in_=hid[h][:].rearrange("p o t -> p (o t)")
+            )
+
+        p_sb = [sb.tile([P, O], F32, name=f"p_sb{n}") for n in range(N // P)]
+        for h in range(2):
+            for n in range(N // P):
+                acc = psum.tile([P, HALF], F32, name=f"bank{(6 + 2 * h + n) % 8}")
+                nc.tensor.matmul_mx(
+                    out=acc[:],
+                    lhsT=vg[:, n * P : (n + 1) * P].bitcast(E4M3X4), lhsT_scale=vg_sc[:, n * P : (n + 1) * P],
+                    rhs=hq[h][:].bitcast(E5M2X4), rhs_scale=hq_sc[h][:],
+                    start=True, stop=True,
+                )
+                dst = p_sb[n][:, h * HALF : (h + 1) * HALF]
+                if h == 1 and n == 1:
+                    nc.vector.tensor_copy(dst, acc[:])
+                else:
+                    nc.scalar.copy(dst, acc[:])
+
+        ends = [sb.tile([P, U], F32, name=f"ends{n}") for n in range(N // P)]
+        for n in range(N // P):
+            nc.scalar.activation(ends[n][:], p_sb[n][:].indirect(idx6[:]), ACT.Copy, scale=so_t[:, n : n + 1])
+        nc.vector.tensor_copy(pages[0][:].indirect(idx7[:]), ends[0][:])
+        nc.scalar.activation(pages[1][:].indirect(idx7[:]), ends[1][:], ACT.Copy)
+        nc.sync.dma_start(out[0:P, :], pages[0][:])
+        nc.scalar.dma_start(out[P : 2 * P, :], pages[1][:])

@@ -13,12 +13,13 @@ E4M3X4 = mybir.dt.float8_e4m3fn_x4
 E5M2X4 = mybir.dt.float8_e5m2_x4
 ACT = mybir.ActivationFunctionType
 
+K, T, J, R, C, O, N, S, U, E = 512, 1024, 256, 512, 512, 256, 256, 1024, 128, 512
 P = 128
 PACK = 4
-K, T, J, R, C, O, N, S, U, E = 512, 1024, 256, 512, 512, 256, 256, 1024, 128, 512
 HALF = 128
 LIST_ROWS = 16
 QUADRANT = 32
+SCALE_ROWS = 4
 
 FLOPS = 2 * K * R * J + 2 * R * N * O
 
@@ -31,39 +32,38 @@ def tile_list_gatedgroupboard_solo_store_postedout_kernel(
     with ExitStack() as ctx:
         lists = ctx.enter_context(tc.tile_pool(name="lists", bufs=1))
         sb = ctx.enter_context(tc.tile_pool(name="sb", bufs=1))
-        reuse = ctx.enter_context(tc.tile_pool(name="reuse", bufs=1))
+        board_pool = ctx.enter_context(tc.tile_pool(name="board_pool", bufs=1))
+        page_pool = ctx.enter_context(tc.tile_pool(name="page_pool", bufs=1))
+        picked_pool = ctx.enter_context(tc.tile_pool(name="picked_pool", bufs=1))
+        store_pool = ctx.enter_context(tc.tile_pool(name="store_pool", bufs=1))
         psum = ctx.enter_context(tc.psum_pool(name="psum", bufs=1))
 
         def load_list(name, src):
-            t = lists.tile(list(src.shape), U16, name=name)
-            nc.sync.dma_start(t[:], src)
-            return t
+            tile = lists.tile(list(src.shape), U16, name=name)
+            nc.sync.dma_start(tile[:], src)
+            return tile
 
         def load_plane(plane, scales):
-            for q in range(4):
+            for q in range(P // QUADRANT):
                 nc.sync.dma_start(
-                    plane[QUADRANT * q : QUADRANT * q + 4, :].bitcast(I32),
-                    scales[0, 4 * q : 4 * q + 4, :].bitcast(I32),
+                    plane[QUADRANT * q : QUADRANT * q + SCALE_ROWS, :].bitcast(I32),
+                    scales[0, SCALE_ROWS * q : SCALE_ROWS * (q + 1), :].bitcast(I32),
                 )
 
-        def half_of(lst, h):
-            return lst[:, h * HALF // LIST_ROWS : (h + 1) * HALF // LIST_ROWS]
+        def entries(lst, first, last):
+            return lst[:, first // LIST_ROWS : last // LIST_ROWS]
 
         xt_plane = sb.tile([P, T], U8, name="xt_plane")
         w_plane = sb.tile([P, R], U8, name="w_plane")
-        vs_plane = sb.tile([P, S], U8, name="vs_plane")
-        boards = [sb.tile([P, C], F32, name=f"board{t}") for t in range(PACK)]
-        pages = [sb.tile([P, E], F32, name=f"page{n}") for n in range(N // P)]
-        nc.vector.memset(xt_plane[:].bitcast(I32), 0)
-        nc.vector.memset(w_plane[:].bitcast(I32), 0)
+        vs_plane = store_pool.tile([P, S], U8, name="vs_plane", offset=0)
+        boards = [sb.tile([P, C], F32, name=f"board{t}") for t in range(2)]
+        for plane in (xt_plane, w_plane, vs_plane):
+            nc.vector.memset(plane[:].bitcast(I32), 0)
         for board in boards:
             nc.vector.memset(board[:], 0.0)
 
-        nc.gpsimd.memset(vs_plane[:].bitcast(I32), 0)
-        for page in pages:
-            nc.gpsimd.memset(page[:], 0.0)
-        w_rows = sb.tile([PACK, 4, R // 4], I32, name="w_rows")
-        nc.sync.dma_start(w_rows[:], w_scales[0].bitcast(I32).rearrange("(q r) c -> r q c", r=4))
+        w_rows = sb.tile([SCALE_ROWS, P // QUADRANT, R // 4], I32, name="w_rows")
+        nc.sync.dma_start(w_rows[:], w_scales[0].bitcast(I32).rearrange("(q r) c -> r q c", r=SCALE_ROWS))
         idx = load_list("idx", offs)
         xt_tab = sb.tile([P, T], U16, name="xt_tab")
         nc.sync.dma_start(xt_tab[:].bitcast(I32), xt_words[0].bitcast(I32))
@@ -78,89 +78,105 @@ def tile_list_gatedgroupboard_solo_store_postedout_kernel(
         sa_t = sb.tile([P, PACK], F32, name="sa_t")
         for dst, src in ((sg_t, sg), (bg_t, bg), (sa_t, sa)):
             nc.sync.dma_start(dst[:], src.rearrange("(p t) one -> p (t one)", t=PACK))
-        vs_tab = sb.tile([P, S], I32, name="vs_tab")
+        vs_tab = store_pool.tile([P, S], I32, name="vs_tab", offset=S)
         nc.sync.dma_start(vs_tab[:], vs_words[0].rearrange("p c b -> p (c b)").bitcast(I32))
         idx5 = load_list("idx5", offs5)
         load_plane(vs_plane, vs_scales)
         idx6 = load_list("idx6", offs6)
         idx7 = load_list("idx7", offs7)
         so_t = sb.tile([P, N // P], F32, name="so_t")
-        with nc.allow_non_contiguous_dma(reason="one value a partition"):
+        with nc.allow_non_contiguous_dma(reason="one value a partition for each block of 128 rows"):
             nc.sync.dma_start(so_t[:], so.rearrange("(a p) one -> p (a one)", p=P))
 
-        for q in range(4):
-            nc.vector.tensor_copy(w_plane[QUADRANT * q : QUADRANT * q + 4, :].bitcast(I32), w_rows[:, q, :])
+        for q in range(P // QUADRANT):
+            nc.vector.tensor_copy(
+                w_plane[QUADRANT * q : QUADRANT * q + SCALE_ROWS, :].bitcast(I32), w_rows[:, q, :]
+            )
         w_sc = sb.tile([P, PACK, P], U8, name="w_sc", align_bytes=64)
-        nc.vector.tensor_copy(
-            w_sc[:].rearrange("p t m -> p m t"), w_plane[:].rearrange("p (m t) -> p m t", t=PACK)
-        )
-        w_q = sb.tile([P, PACK, P], U32, name="w_q", align_bytes=64)
-        nc.scalar.copy(
-            w_q[:].rearrange("p t m -> p m t"), w_raw[:].bitcast(U32).rearrange("p (m t) -> p m t", t=PACK)
-        )
+        w_q = [sb.tile([P, n, P], U32, name=f"w_q{n}", align_bytes=64) for n in (1, PACK - 1)]
+        w_plane_mt = w_plane[:].rearrange("p (m t) -> p m t", t=PACK)
+        w_raw_mt = w_raw[:].bitcast(U32).rearrange("p (m t) -> p m t", t=PACK)
+        nc.vector.tensor_copy(w_sc[:].rearrange("p t m -> p m t"), w_plane_mt)
+        nc.scalar.copy(w_q[0][:].rearrange("p t m -> p m t"), w_raw_mt[:, :, 0:1])
+        nc.scalar.copy(w_q[1][:].rearrange("p t m -> p m t"), w_raw_mt[:, :, 1:PACK])
 
         xg = sb.tile([P, J], U16, name="xg", align_bytes=64)
         xg_sc = sb.tile([P, J], U8, name="xg_sc", align_bytes=64)
-        for h in range(2):
-            cols = slice(h * HALF, (h + 1) * HALF)
-            nc.vector.tensor_copy(xg[:, cols], xt_tab[:].indirect(half_of(idx, h)))
-            nc.vector.tensor_copy(xg_sc[:, cols], xt_plane[:].indirect(half_of(idx, h)))
+        for j0 in range(0, J, HALF):
+            nc.vector.tensor_copy(xg[:, j0 : j0 + HALF], xt_tab[:].indirect(entries(idx, j0, j0 + HALF)))
+            nc.vector.tensor_copy(xg_sc[:, j0 : j0 + HALF], xt_plane[:].indirect(entries(idx, j0, j0 + HALF)))
+        w_codes = [w_q[0][:, 0, :]] + [w_q[1][:, t, :] for t in range(PACK - 1)]
 
-        a_sb = [sb.tile([P, J], F32, name=f"a_sb{t}") for t in range(PACK - 1)]
-        a_sb.append(reuse.tile([P, J], F32, name="a_last", offset=0, align_bytes=64))
-        steps = [(0, 0, 128), (0, 128, 256), (1, 0, 256), (2, 0, 256), (3, 0, 256)]
-        for i, (t, j0, j1) in enumerate(steps):
-            acc = psum.tile([P, j1 - j0], F32, name=f"bank{i}")
-            nc.tensor.matmul_mx(
-                out=acc[:],
-                lhsT=w_q[:, t, :].bitcast(E5M2X4), lhsT_scale=w_sc[:, t, :],
-                rhs=xg[:, j0:j1].bitcast(E2M1X4), rhs_scale=xg_sc[:, j0:j1],
-                start=True, stop=True,
-            )
-            nc.scalar.copy(a_sb[t][:, j0:j1], acc[:])
-        for t, j0, j1 in steps:
-            nc.vector.tensor_copy(
-                boards[t][:].indirect(idx2[:, j0 // LIST_ROWS : j1 // LIST_ROWS]), a_sb[t][:, j0:j1]
-            )
-
-        gate = sb.tile([P, PACK, O], F32, name="gate")
-        val = sb.tile([P, PACK, O], F32, name="val")
-        for t in range(PACK):
-            for o0, o1 in ((0, HALF), (HALF, O)) if t == PACK - 1 else ((0, O),):
-                entries = slice(o0 // LIST_ROWS, o1 // LIST_ROWS)
-                nc.scalar.activation(
-                    gate[:, t, o0:o1], boards[t][:].indirect(idx4[:, entries]), ACT.Sigmoid,
-                    bias=bg_t[:, t : t + 1], scale=sg_t[:, t : t + 1],
+        groups = [[(0, 0, HALF)], [(0, HALF, J)], [(1, 0, J)], [(2, 0, J), (3, 0, J)]]
+        a_sb = [
+            board_pool.tile([P, HALF], F32, name="a_sb0", offset=4 * C - 2 * HALF),
+            page_pool.tile([P, HALF], F32, name="a_sb1", offset=4 * E - 2 * HALF),
+            sb.tile([P, J], F32, name="a_sb2"),
+            picked_pool.tile([P, 2 * J], F32, name="a_sb3", offset=0, align_bytes=64),
+        ]
+        puts = []
+        for g, group in enumerate(groups):
+            acc = psum.tile(list(a_sb[g].shape), F32, name=f"bank{g}")
+            col = 0
+            for t, j0, j1 in group:
+                cols = slice(col, col + j1 - j0)
+                nc.tensor.matmul_mx(
+                    out=acc[:, cols],
+                    lhsT=w_codes[t].bitcast(E5M2X4), lhsT_scale=w_sc[:, t, :],
+                    rhs=xg[:, j0:j1].bitcast(E2M1X4), rhs_scale=xg_sc[:, j0:j1],
+                    start=True, stop=True,
                 )
-                nc.scalar.activation(
-                    val[:, t, o0:o1], boards[t][:].indirect(idx3[:, entries]), ACT.Copy,
-                    scale=sa_t[:, t : t + 1],
-                )
+                puts.append((t, j0, j1, a_sb[g][:, cols]))
+                col = cols.stop
+            nc.scalar.copy(a_sb[g][:], acc[:])
+        for t, j0, j1, values in puts:
+            if t == len(boards):
+                boards.append(board_pool.tile([P, C], F32, name=f"board{t}", offset=4 * C * (t - 2)))
+                nc.gpsimd.memset(boards[t][:], 0.0)
+            nc.vector.tensor_copy(boards[t][:].indirect(entries(idx2, j0, j1)), values)
 
-        vg = reuse.tile([P, N], U32, name="vg", offset=N, align_bytes=64)
-        vg_sc = reuse.tile([P, N], U8, name="vg_sc", offset=0, align_bytes=64)
+        pages = [page_pool.tile([P, E], F32, name=f"page{n}", offset=4 * E * n) for n in range(N // P)]
+        for page in pages:
+            nc.gpsimd.memset(page[:], 0.0)
+
+        gate = sb.tile([P, PACK * O], F32, name="gate")
+        val = sb.tile([P, PACK * O], F32, name="val")
+        looks = [(t, 0, O) for t in range(PACK - 1)] + [(PACK - 1, 0, HALF), (PACK - 1, HALF, O)]
+        for t, o0, o1 in looks:
+            nc.scalar.activation(
+                gate[:, t * O + o0 : t * O + o1], boards[t][:].indirect(entries(idx4, o0, o1)), ACT.Sigmoid,
+                bias=bg_t[:, t : t + 1], scale=sg_t[:, t : t + 1],
+            )
+            nc.scalar.activation(
+                val[:, t * O + o0 : t * O + o1], boards[t][:].indirect(entries(idx3, o0, o1)), ACT.Copy,
+                scale=sa_t[:, t : t + 1],
+            )
+
+        vg = picked_pool.tile([P, N], U32, name="vg", offset=N, align_bytes=64)
+        vg_sc = picked_pool.tile([P, N], U8, name="vg_sc", offset=0, align_bytes=64)
         nc.vector.tensor_copy(vg[:], vs_tab[:].bitcast(U32).indirect(idx5[:]))
         nc.vector.tensor_copy(vg_sc[:], vs_plane[:].indirect(idx5[:]))
 
-        hid = [sb.tile([P, HALF, PACK], BF16, name=f"hid{h}", align_bytes=64) for h in range(2)]
+        hid_all = store_pool.tile([P, O * PACK], BF16, name="hid_all", offset=S // 2, align_bytes=64)
+        hid = [hid_all[:, h * HALF * PACK : (h + 1) * HALF * PACK] for h in range(2)]
         hq = [sb.tile([P, HALF], U32, name=f"hq{h}", align_bytes=64) for h in range(2)]
         hq_sc = [sb.tile([P, HALF], U8, name=f"hq_sc{h}", align_bytes=64) for h in range(2)]
         for h in range(2):
             nc.vector.tensor_tensor(
-                hid[h][:].rearrange("p (c i) t -> p c t i", i=4),
-                val[:, :, h * HALF : (h + 1) * HALF].rearrange("p t (c i) -> p c t i", i=4),
-                gate[:, :, h * HALF : (h + 1) * HALF].rearrange("p t (c i) -> p c t i", i=4),
+                hid[h].rearrange("p (c i t) -> p c t i", i=4, t=PACK),
+                val[:].rearrange("p (t h c i) -> p h c t i", t=PACK, h=2, i=4)[:, h],
+                gate[:].rearrange("p (t h c i) -> p h c t i", t=PACK, h=2, i=4)[:, h],
                 mybir.AluOpType.mult,
             )
         for h in range(2):
             nc.vector.quantize_mx(
-                out=hq[h][:].bitcast(E5M2X4), scales=hq_sc[h][:], in_=hid[h][:].rearrange("p o t -> p (o t)")
+                out=hq[h][:].bitcast(E5M2X4), scales=hq_sc[h][:], in_=hid[h]
             )
 
         p_sb = [sb.tile([P, O], F32, name=f"p_sb{n}") for n in range(N // P)]
         for h in range(2):
             for n in range(N // P):
-                acc = psum.tile([P, HALF], F32, name=f"bank{(6 + 2 * h + n) % 8}")
+                acc = psum.tile([P, HALF], F32, name=f"bank{len(groups) + 2 * h + n}")
                 nc.tensor.matmul_mx(
                     out=acc[:],
                     lhsT=vg[:, n * P : (n + 1) * P].bitcast(E4M3X4), lhsT_scale=vg_sc[:, n * P : (n + 1) * P],
@@ -168,7 +184,7 @@ def tile_list_gatedgroupboard_solo_store_postedout_kernel(
                     start=True, stop=True,
                 )
                 dst = p_sb[n][:, h * HALF : (h + 1) * HALF]
-                if h == 1 and n == 1:
+                if h == 1 and n == 0:
                     nc.vector.tensor_copy(dst, acc[:])
                 else:
                     nc.scalar.copy(dst, acc[:])

@@ -32,6 +32,7 @@ def tile_list_gatedgroupboard_solo_store_postedout_kernel(
     with ExitStack() as ctx:
         lists = ctx.enter_context(tc.tile_pool(name="lists", bufs=1))
         sb = ctx.enter_context(tc.tile_pool(name="sb", bufs=1))
+        token_pool = ctx.enter_context(tc.tile_pool(name="token_pool", bufs=1))
         board_pool = ctx.enter_context(tc.tile_pool(name="board_pool", bufs=1))
         page_pool = ctx.enter_context(tc.tile_pool(name="page_pool", bufs=1))
         picked_pool = ctx.enter_context(tc.tile_pool(name="picked_pool", bufs=1))
@@ -53,7 +54,7 @@ def tile_list_gatedgroupboard_solo_store_postedout_kernel(
         def entries(lst, first, last):
             return lst[:, first // LIST_ROWS : last // LIST_ROWS]
 
-        xt_plane = sb.tile([P, T], U8, name="xt_plane")
+        xt_plane = token_pool.tile([P, T], U8, name="xt_plane", offset=0)
         w_plane = sb.tile([P, R], U8, name="w_plane")
         vs_plane = store_pool.tile([P, S], U8, name="vs_plane", offset=0)
         boards = [sb.tile([P, C], F32, name=f"board{t}") for t in range(2)]
@@ -92,11 +93,14 @@ def tile_list_gatedgroupboard_solo_store_postedout_kernel(
             nc.vector.tensor_copy(
                 w_plane[QUADRANT * q : QUADRANT * q + SCALE_ROWS, :].bitcast(I32), w_rows[:, q, :]
             )
-        w_sc = sb.tile([P, PACK, P], U8, name="w_sc", align_bytes=64)
+        w_sc = [
+            sb.tile([P, 1, P], U8, name="w_sc_first", align_bytes=64),
+            token_pool.tile([P, PACK - 1, P], U8, name="w_sc_rest", offset=0, align_bytes=64),
+        ]
         w_q = [sb.tile([P, n, P], U32, name=f"w_q{n}", align_bytes=64) for n in (1, PACK - 1)]
-        w_plane_mt = w_plane[:].rearrange("p (m t) -> p m t", t=PACK)
         w_raw_mt = w_raw[:].bitcast(U32).rearrange("p (m t) -> p m t", t=PACK)
-        nc.vector.tensor_copy(w_sc[:].rearrange("p t m -> p m t"), w_plane_mt)
+        w_plane_tm = w_plane[:].rearrange("p (m t) -> p t m", t=PACK)
+        nc.vector.tensor_copy(w_sc[0][:], w_plane_tm[:, 0:1, :])
         nc.scalar.copy(w_q[0][:].rearrange("p t m -> p m t"), w_raw_mt[:, :, 0:1])
         nc.scalar.copy(w_q[1][:].rearrange("p t m -> p m t"), w_raw_mt[:, :, 1:PACK])
 
@@ -105,6 +109,8 @@ def tile_list_gatedgroupboard_solo_store_postedout_kernel(
         for j0 in range(0, J, HALF):
             nc.vector.tensor_copy(xg[:, j0 : j0 + HALF], xt_tab[:].indirect(entries(idx, j0, j0 + HALF)))
             nc.vector.tensor_copy(xg_sc[:, j0 : j0 + HALF], xt_plane[:].indirect(entries(idx, j0, j0 + HALF)))
+        nc.vector.tensor_copy(w_sc[1][:], w_plane_tm[:, 1:PACK, :])
+        w_bytes = [w_sc[0][:, 0, :]] + [w_sc[1][:, t, :] for t in range(PACK - 1)]
         w_codes = [w_q[0][:, 0, :]] + [w_q[1][:, t, :] for t in range(PACK - 1)]
 
         groups = [[(0, 0, HALF)], [(0, HALF, J)], [(1, 0, J)], [(2, 0, J), (3, 0, J)]]
@@ -122,7 +128,7 @@ def tile_list_gatedgroupboard_solo_store_postedout_kernel(
                 cols = slice(col, col + j1 - j0)
                 nc.tensor.matmul_mx(
                     out=acc[:, cols],
-                    lhsT=w_codes[t].bitcast(E5M2X4), lhsT_scale=w_sc[:, t, :],
+                    lhsT=w_codes[t].bitcast(E5M2X4), lhsT_scale=w_bytes[t],
                     rhs=xg[:, j0:j1].bitcast(E2M1X4), rhs_scale=xg_sc[:, j0:j1],
                     start=True, stop=True,
                 )
@@ -163,9 +169,9 @@ def tile_list_gatedgroupboard_solo_store_postedout_kernel(
         hq_sc = [sb.tile([P, HALF], U8, name=f"hq_sc{h}", align_bytes=64) for h in range(2)]
         for h in range(2):
             nc.vector.tensor_tensor(
-                hid[h].rearrange("p (c i t) -> p c t i", i=4, t=PACK),
-                val[:].rearrange("p (t h c i) -> p h c t i", t=PACK, h=2, i=4)[:, h],
-                gate[:].rearrange("p (t h c i) -> p h c t i", t=PACK, h=2, i=4)[:, h],
+                hid[h].rearrange("p (c i t) -> p c t i", i=2, t=PACK),
+                val[:].rearrange("p (t h c i) -> p h c t i", t=PACK, h=2, i=2)[:, h],
+                gate[:].rearrange("p (t h c i) -> p h c t i", t=PACK, h=2, i=2)[:, h],
                 mybir.AluOpType.mult,
             )
         for h in range(2):

from contextlib import ExitStack

import concourse.mybir as mybir

F32 = mybir.dt.float32
BF16 = mybir.dt.bfloat16
I32 = mybir.dt.int32
U32 = mybir.dt.uint32
U16 = mybir.dt.uint16
U8 = mybir.dt.uint8
E2M1X4 = mybir.dt.float4_e2m1fn_x4
E4M3X4 = mybir.dt.float8_e4m3fn_x4
E5M2X4 = mybir.dt.float8_e5m2_x4
ACT = mybir.ActivationFunctionType

K, T, J, R, C, O, N, S, U, E = 512, 1024, 256, 512, 512, 256, 256, 1024, 128, 512
P = 128
PACK = 4
HALF = 128
LIST_ROWS = 16
QUADRANT = 32
SCALE_ROWS = 4

FLOPS = 2 * K * R * J + 2 * R * N * O


def tile_list_gatedgroupboard_solo_store_postedout_kernel(
    tc, xt_words, xt_scales, w_words, w_scales, sa, sg, bg, vs_words, vs_scales, so,
    offs, offs2, offs3, offs4, offs5, offs6, offs7, out,
):
    nc = tc.nc
    with ExitStack() as ctx:
        lists = ctx.enter_context(tc.tile_pool(name="lists", bufs=1))
        sb = ctx.enter_context(tc.tile_pool(name="sb", bufs=1))
        token_pool = ctx.enter_context(tc.tile_pool(name="token_pool", bufs=1))
        board_pool = ctx.enter_context(tc.tile_pool(name="board_pool", bufs=1))
        page_pool = ctx.enter_context(tc.tile_pool(name="page_pool", bufs=1))
        picked_pool = ctx.enter_context(tc.tile_pool(name="picked_pool", bufs=1))
        store_pool = ctx.enter_context(tc.tile_pool(name="store_pool", bufs=1))
        psum = ctx.enter_context(tc.psum_pool(name="psum", bufs=1))

        def load_list(name, src):
            tile = lists.tile(list(src.shape), U16, name=name)
            nc.sync.dma_start(tile[:], src)
            return tile

        def load_plane(plane, scales):
            for q in range(P // QUADRANT):
                nc.sync.dma_start(
                    plane[QUADRANT * q : QUADRANT * q + SCALE_ROWS, :].bitcast(I32),
                    scales[0, SCALE_ROWS * q : SCALE_ROWS * (q + 1), :].bitcast(I32),
                )

        def entries(lst, first, last):
            return lst[:, first // LIST_ROWS : last // LIST_ROWS]

        xt_plane = token_pool.tile([P, T], U8, name="xt_plane", offset=0)
        w_plane = sb.tile([P, R], U8, name="w_plane")
        vs_plane = store_pool.tile([P, S], U8, name="vs_plane", offset=0)
        boards = [sb.tile([P, C], F32, name=f"board{t}") for t in range(2)]
        for plane in (xt_plane, w_plane, vs_plane):
            nc.vector.memset(plane[:].bitcast(I32), 0)
        for board in boards:
            nc.vector.memset(board[:], 0.0)

        w_rows = sb.tile([SCALE_ROWS, P // QUADRANT, R // 4], I32, name="w_rows")
        nc.sync.dma_start(w_rows[:], w_scales[0].bitcast(I32).rearrange("(q r) c -> r q c", r=SCALE_ROWS))
        idx = load_list("idx", offs)
        xt_tab = sb.tile([P, T], U16, name="xt_tab")
        nc.sync.dma_start(xt_tab[:].bitcast(I32), xt_words[0].bitcast(I32))
        w_raw = sb.tile([P, R], I32, name="w_raw")
        nc.sync.dma_start(w_raw[:], w_words[0].rearrange("p c b -> p (c b)").bitcast(I32))
        load_plane(xt_plane, xt_scales)
        idx2 = load_list("idx2", offs2)
        idx4 = load_list("idx4", offs4)
        idx3 = load_list("idx3", offs3)
        sg_t = sb.tile([P, PACK], F32, name="sg_t")
        bg_t = sb.tile([P, PACK], F32, name="bg_t")
        sa_t = sb.tile([P, PACK], F32, name="sa_t")
        for dst, src in ((sg_t, sg), (bg_t, bg), (sa_t, sa)):
            nc.sync.dma_start(dst[:], src.rearrange("(p t) one -> p (t one)", t=PACK))
        vs_tab = store_pool.tile([P, S], I32, name="vs_tab", offset=S)
        nc.sync.dma_start(vs_tab[:], vs_words[0].rearrange("p c b -> p (c b)").bitcast(I32))
        idx5 = load_list("idx5", offs5)
        load_plane(vs_plane, vs_scales)
        idx6 = load_list("idx6", offs6)
        idx7 = load_list("idx7", offs7)
        so_t = sb.tile([P, N // P], F32, name="so_t")
        with nc.allow_non_contiguous_dma(reason="one value a partition for each block of 128 rows"):
            nc.sync.dma_start(so_t[:], so.rearrange("(a p) one -> p (a one)", p=P))

        for q in range(P // QUADRANT):
            nc.vector.tensor_copy(
                w_plane[QUADRANT * q : QUADRANT * q + SCALE_ROWS, :].bitcast(I32), w_rows[:, q, :]
            )
        w_sc = [
            sb.tile([P, 1, P], U8, name="w_sc_first", align_bytes=64),
            token_pool.tile([P, PACK - 1, P], U8, name="w_sc_rest", offset=0, align_bytes=64),
        ]
        w_q = [sb.tile([P, n, P], U32, name=f"w_q{n}", align_bytes=64) for n in (1, PACK - 1)]
        w_raw_mt = w_raw[:].bitcast(U32).rearrange("p (m t) -> p m t", t=PACK)
        w_plane_tm = w_plane[:].rearrange("p (m t) -> p t m", t=PACK)
        nc.vector.tensor_copy(w_sc[0][:], w_plane_tm[:, 0:1, :])
        nc.scalar.copy(w_q[0][:].rearrange("p t m -> p m t"), w_raw_mt[:, :, 0:1])
        nc.scalar.copy(w_q[1][:].rearrange("p t m -> p m t"), w_raw_mt[:, :, 1:PACK])

        xg = sb.tile([P, J], U16, name="xg", align_bytes=64)
        xg_sc = sb.tile([P, J], U8, name="xg_sc", align_bytes=64)
        for j0 in range(0, J, HALF):
            nc.vector.tensor_copy(xg[:, j0 : j0 + HALF], xt_tab[:].indirect(entries(idx, j0, j0 + HALF)))
            nc.vector.tensor_copy(xg_sc[:, j0 : j0 + HALF], xt_plane[:].indirect(entries(idx, j0, j0 + HALF)))
        nc.vector.tensor_copy(w_sc[1][:], w_plane_tm[:, 1:PACK, :])
        w_bytes = [w_sc[0][:, 0, :]] + [w_sc[1][:, t, :] for t in range(PACK - 1)]
        w_codes = [w_q[0][:, 0, :]] + [w_q[1][:, t, :] for t in range(PACK - 1)]

        groups = [[(0, 0, HALF)], [(0, HALF, J)], [(1, 0, J)], [(2, 0, J), (3, 0, J)]]
        a_sb = [
            board_pool.tile([P, HALF], F32, name="a_sb0", offset=4 * C - 2 * HALF),
            page_pool.tile([P, HALF], F32, name="a_sb1", offset=4 * E - 2 * HALF),
            sb.tile([P, J], F32, name="a_sb2"),
            picked_pool.tile([P, 2 * J], F32, name="a_sb3", offset=0, align_bytes=64),
        ]
        puts = []
        for g, group in enumerate(groups):
            acc = psum.tile(list(a_sb[g].shape), F32, name=f"bank{g}")
            col = 0
            for t, j0, j1 in group:
                cols = slice(col, col + j1 - j0)
                nc.tensor.matmul_mx(
                    out=acc[:, cols],
                    lhsT=w_codes[t].bitcast(E5M2X4), lhsT_scale=w_bytes[t],
                    rhs=xg[:, j0:j1].bitcast(E2M1X4), rhs_scale=xg_sc[:, j0:j1],
                    start=True, stop=True,
                )
                puts.append((t, j0, j1, a_sb[g][:, cols]))
                col = cols.stop
            nc.scalar.copy(a_sb[g][:], acc[:])
        for t, j0, j1, values in puts:
            if t == len(boards):
                boards.append(board_pool.tile([P, C], F32, name=f"board{t}", offset=4 * C * (t - 2)))
                nc.gpsimd.memset(boards[t][:], 0.0)
            nc.vector.tensor_copy(boards[t][:].indirect(entries(idx2, j0, j1)), values)

        pages = [page_pool.tile([P, E], F32, name=f"page{n}", offset=4 * E * n) for n in range(N // P)]
        for page in pages:
            nc.gpsimd.memset(page[:], 0.0)

        gate = sb.tile([P, PACK * O], F32, name="gate")
        val = sb.tile([P, PACK * O], F32, name="val")
        looks = [(t, 0, O) for t in range(PACK - 1)] + [(PACK - 1, 0, HALF), (PACK - 1, HALF, O)]
        for t, o0, o1 in looks:
            nc.scalar.activation(
                gate[:, t * O + o0 : t * O + o1], boards[t][:].indirect(entries(idx4, o0, o1)), ACT.Sigmoid,
                bias=bg_t[:, t : t + 1], scale=sg_t[:, t : t + 1],
            )
            nc.scalar.activation(
                val[:, t * O + o0 : t * O + o1], boards[t][:].indirect(entries(idx3, o0, o1)), ACT.Copy,
                scale=sa_t[:, t : t + 1],
            )

        vg = picked_pool.tile([P, N], U32, name="vg", offset=N, align_bytes=64)
        vg_sc = picked_pool.tile([P, N], U8, name="vg_sc", offset=0, align_bytes=64)
        nc.vector.tensor_copy(vg[:], vs_tab[:].bitcast(U32).indirect(idx5[:]))
        nc.vector.tensor_copy(vg_sc[:], vs_plane[:].indirect(idx5[:]))

        hid_all = store_pool.tile([P, O * PACK], BF16, name="hid_all", offset=S // 2, align_bytes=64)
        hid = [hid_all[:, h * HALF * PACK : (h + 1) * HALF * PACK] for h in range(2)]
        hq = [sb.tile([P, HALF], U32, name=f"hq{h}", align_bytes=64) for h in range(2)]
        hq_sc = [sb.tile([P, HALF], U8, name=f"hq_sc{h}", align_bytes=64) for h in range(2)]
        for h in range(2):
            nc.vector.tensor_tensor(
                hid[h].rearrange("p (c i t) -> p c t i", i=2, t=PACK),
                val[:].rearrange("p (t h c i) -> p h c t i", t=PACK, h=2, i=2)[:, h],
                gate[:].rearrange("p (t h c i) -> p h c t i", t=PACK, h=2, i=2)[:, h],
                mybir.AluOpType.mult,
            )
        for h in range(2):
            nc.vector.quantize_mx(
                out=hq[h][:].bitcast(E5M2X4), scales=hq_sc[h][:], in_=hid[h]
            )

        p_sb = [sb.tile([P, O], F32, name=f"p_sb{n}") for n in range(N // P)]
        for h in range(2):
            for n in range(N // P):
                acc = psum.tile([P, HALF], F32, name=f"bank{len(groups) + 2 * h + n}")
                nc.tensor.matmul_mx(
                    out=acc[:],
                    lhsT=vg[:, n * P : (n + 1) * P].bitcast(E4M3X4), lhsT_scale=vg_sc[:, n * P : (n + 1) * P],
                    rhs=hq[h][:].bitcast(E5M2X4), rhs_scale=hq_sc[h][:],
                    start=True, stop=True,
                )
                dst = p_sb[n][:, h * HALF : (h + 1) * HALF]
                if h == 1 and n == 0:
                    nc.vector.tensor_copy(dst, acc[:])
                else:
                    nc.scalar.copy(dst, acc[:])

        ends = [sb.tile([P, U], F32, name=f"ends{n}") for n in range(N // P)]
        for n in range(N // P):
            nc.scalar.activation(ends[n][:], p_sb[n][:].indirect(idx6[:]), ACT.Copy, scale=so_t[:, n : n + 1])
        nc.vector.tensor_copy(pages[0][:].indirect(idx7[:]), ends[0][:])
        nc.scalar.activation(pages[1][:].indirect(idx7[:]), ends[1][:], ACT.Copy)
        nc.sync.dma_start(out[0:P, :], pages[0][:])
        nc.scalar.dma_start(out[P : 2 * P, :], pages[1][:])
